import numpy as np
import ml_dtypes

BF16 = ml_dtypes.bfloat16


def bf(x):
    return np.asarray(x, np.float32).astype(BF16)


def f32(x):
    return np.asarray(x, np.float32)


def f64(x):
    return np.asarray(x).astype(np.float64)


def striped(idx):
    return np.tile(idx.reshape(-1, 16).T, (8, 1))


S, K, M, N, D, V = 1024, 128, 512, 512, 16, 32


def sigmoid(v):
    return 1.0 / (1.0 + np.exp(-v))


def setup_inputs():
    return {"table": bf(np.random.standard_normal((K, S))), "w": bf(np.random.standard_normal((K, M)) / np.sqrt(K)), "b": f32(0.5 * np.random.standard_normal((M, 1))), "offs": striped(np.random.permutation(np.tile(np.arange(S), 2))[:N])}


def reference(table, w, b, offs):
    idx = offs[:16].T.reshape(-1)
    x = f64(table)[:, idx]
    y = f64(w).T @ x
    z = (y + f64(b)) * sigmoid(y + f64(b))
    return z.reshape(M, V, D).max(axis=2)

@@ -1,0 +1,53 @@
+import concourse.mybir as mybir
+
+BF16, F32, U16 = mybir.dt.bfloat16, mybir.dt.float32, mybir.dt.uint16
+
+P = 128
+S = 1024
+M = 512
+N = 512
+D = 16
+V = N // D
+BLOCKS = M // P
+
+FLOPS = 2 * P * M * N
+
+
+def tile_gather_matmul_kernel(tc, table, w, b, offs, out):
+    nc = tc.nc
+    with (
+        tc.tile_pool(name="held", bufs=1) as held,
+        tc.tile_pool(name="work", bufs=2) as work,
+        tc.psum_pool(name="psum", bufs=BLOCKS) as psum,
+    ):
+        offsets = held.tile([P, N // 16], U16, name="offsets")
+        nc.sync.dma_start(offsets[:], offs)
+        nodes = held.tile([P, S], BF16, name="nodes")
+        nc.sync.dma_start(nodes[:], table)
+        weights = held.tile([P, M], BF16, name="weights")
+        nc.scalar.dma_start(weights[:], w)
+        bias = held.tile([P, BLOCKS], F32, name="bias")
+        with nc.allow_non_contiguous_dma(reason="512 single values, one to a partition and block"):
+            nc.scalar.dma_start(bias[:], b.rearrange("(a p) o -> p (a o)", p=P))
+
+        pooled = held.tile([P, BLOCKS, V], F32, name="pooled")
+        for a in range(BLOCKS):
+            y = psum.tile([P, N], F32, name="y")
+            nc.tensor.matmul(
+                y[:],
+                weights[:, a * P : (a + 1) * P],
+                nodes[:].indirect(offsets[:]),
+                start=True,
+                stop=True,
+            )
+            z = work.tile([P, N], F32, name="z")
+            nc.scalar.activation(
+                z[:], y[:], mybir.ActivationFunctionType.Silu, bias=bias[:, a : a + 1]
+            )
+            nc.vector.tensor_reduce(
+                pooled[:, a, :],
+                z[:].rearrange("p (v t) -> p v t", t=D),
+                axis=mybir.AxisListType.X,
+                op=mybir.AluOpType.max,
+            )
+        nc.sync.dma_start(out.rearrange("(a p) v -> p a v", p=P), pooled[:])

@@ -30,6 +30,10 @@ def tile_gather_matmul_kernel(tc, table, w, b, offs, out):
         with nc.allow_non_contiguous_dma(reason="512 single values, one to a partition and block"):
             nc.scalar.dma_start(bias[:], b.rearrange("(a p) o -> p (a o)", p=P))
 
+        early = held.tile([P, 2], F32, name="early")
+        nc.vector.memset(early[:, 0:1], 0.0)
+        nc.scalar.activation(early[:, 1:2], early[:, 0:1], mybir.ActivationFunctionType.Silu)
+
         pooled = held.tile([P, BLOCKS, V], F32, name="pooled")
         for a in range(BLOCKS):
             y = psum.tile([P, N], F32, name="y")

@@ -9,6 +9,7 @@ N = 512
 D = 16
 V = N // D
 BLOCKS = M // P
+WARM = 4
 
 FLOPS = 2 * P * M * N
 
@@ -19,6 +20,7 @@ def tile_gather_matmul_kernel(tc, table, w, b, offs, out):
         tc.tile_pool(name="held", bufs=1) as held,
         tc.tile_pool(name="work", bufs=2) as work,
         tc.psum_pool(name="psum", bufs=BLOCKS) as psum,
+        tc.psum_pool(name="spare", bufs=1) as spare,
     ):
         offsets = held.tile([P, N // 16], U16, name="offsets")
         nc.sync.dma_start(offsets[:], offs)
@@ -29,6 +31,12 @@ def tile_gather_matmul_kernel(tc, table, w, b, offs, out):
         bias = held.tile([P, BLOCKS], F32, name="bias")
         with nc.allow_non_contiguous_dma(reason="512 single values, one to a partition and block"):
             nc.scalar.dma_start(bias[:], b.rearrange("(a p) o -> p (a o)", p=P))
+
+        zeros = held.tile([P, N], BF16, name="zeros")
+        nc.vector.memset(zeros[:], 0.0)
+        unread = spare.tile([P, N], F32, name="unread")
+        for i in range(WARM):
+            nc.tensor.matmul(unread[:], zeros[:, 0:P], zeros[:], start=True, stop=True)
 
         early = held.tile([P, 2], F32, name="early")
         nc.vector.memset(early[:, 0:1], 0.0)

@@ -9,7 +9,7 @@ N = 512
 D = 16
 V = N // D
 BLOCKS = M // P
-WARM = 4
+PIECES = BLOCKS + 2
 
 FLOPS = 2 * P * M * N
 
@@ -18,9 +18,8 @@ def tile_gather_matmul_kernel(tc, table, w, b, offs, out):
     nc = tc.nc
     with (
         tc.tile_pool(name="held", bufs=1) as held,
-        tc.tile_pool(name="work", bufs=2) as work,
-        tc.psum_pool(name="psum", bufs=BLOCKS) as psum,
-        tc.psum_pool(name="spare", bufs=1) as spare,
+        tc.tile_pool(name="work", bufs=PIECES) as work,
+        tc.psum_pool(name="psum", bufs=PIECES) as psum,
     ):
         offsets = held.tile([P, N // 16], U16, name="offsets")
         nc.sync.dma_start(offsets[:], offs)
@@ -32,34 +31,31 @@ def tile_gather_matmul_kernel(tc, table, w, b, offs, out):
         with nc.allow_non_contiguous_dma(reason="512 single values, one to a partition and block"):
             nc.scalar.dma_start(bias[:], b.rearrange("(a p) o -> p (a o)", p=P))
 
-        zeros = held.tile([P, N], BF16, name="zeros")
-        nc.vector.memset(zeros[:], 0.0)
-        unread = spare.tile([P, N], F32, name="unread")
-        for i in range(WARM):
-            nc.tensor.matmul(unread[:], zeros[:, 0:P], zeros[:], start=True, stop=True)
-
         early = held.tile([P, 2], F32, name="early")
         nc.vector.memset(early[:, 0:1], 0.0)
         nc.scalar.activation(early[:, 1:2], early[:, 0:1], mybir.ActivationFunctionType.Silu)
 
         pooled = held.tile([P, BLOCKS, V], F32, name="pooled")
         for a in range(BLOCKS):
-            y = psum.tile([P, N], F32, name="y")
-            nc.tensor.matmul(
-                y[:],
-                weights[:, a * P : (a + 1) * P],
-                nodes[:].indirect(offsets[:]),
-                start=True,
-                stop=True,
-            )
-            z = work.tile([P, N], F32, name="z")
-            nc.scalar.activation(
-                z[:], y[:], mybir.ActivationFunctionType.Silu, bias=bias[:, a : a + 1]
-            )
-            nc.vector.tensor_reduce(
-                pooled[:, a, :],
-                z[:].rearrange("p (v t) -> p v t", t=D),
-                axis=mybir.AxisListType.X,
-                op=mybir.AluOpType.max,
-            )
-        nc.sync.dma_start(out.rearrange("(a p) v -> p a v", p=P), pooled[:])
+            halves = 2 if a in (0, BLOCKS - 1) else 1
+            width = N // halves
+            for h in range(halves):
+                y = psum.tile([P, width], F32, name="y")
+                nc.tensor.matmul(
+                    y[:],
+                    weights[:, a * P : (a + 1) * P],
+                    nodes[:].indirect(offsets[:, h * width // 16 : (h + 1) * width // 16]),
+                    start=True,
+                    stop=True,
+                )
+                z = work.tile([P, width], F32, name="z")
+                nc.scalar.activation(
+                    z[:], y[:], mybir.ActivationFunctionType.Silu, bias=bias[:, a : a + 1]
+                )
+                nc.vector.tensor_reduce(
+                    pooled[:, a, h * width // D : (h + 1) * width // D],
+                    z[:].rearrange("p (v t) -> p v t", t=D),
+                    axis=mybir.AxisListType.X,
+                    op=mybir.AluOpType.max,
+                )
+            nc.sync.dma_start(out[a * P : (a + 1) * P, :], pooled[:, a, :])

@@ -9,7 +9,8 @@ N = 512
 D = 16
 V = N // D
 BLOCKS = M // P
-PIECES = BLOCKS + 2
+HALVES = 2
+PIECES = BLOCKS * HALVES
 
 FLOPS = 2 * P * M * N
 
@@ -37,9 +38,8 @@ def tile_gather_matmul_kernel(tc, table, w, b, offs, out):
 
         pooled = held.tile([P, BLOCKS, V], F32, name="pooled")
         for a in range(BLOCKS):
-            halves = 2 if a in (0, BLOCKS - 1) else 1
-            width = N // halves
-            for h in range(halves):
+            width = N // HALVES
+            for h in range(HALVES):
                 y = psum.tile([P, width], F32, name="y")
                 nc.tensor.matmul(
                     y[:],

@@ -9,8 +9,9 @@ N = 512
 D = 16
 V = N // D
 BLOCKS = M // P
-HALVES = 2
-PIECES = BLOCKS * HALVES
+QUARTERS = 4
+PIECES = BLOCKS * QUARTERS
+BANKS = 8
 
 FLOPS = 2 * P * M * N
 
@@ -20,7 +21,7 @@ def tile_gather_matmul_kernel(tc, table, w, b, offs, out):
     with (
         tc.tile_pool(name="held", bufs=1) as held,
         tc.tile_pool(name="work", bufs=PIECES) as work,
-        tc.psum_pool(name="psum", bufs=PIECES) as psum,
+        tc.psum_pool(name="psum", bufs=BANKS) as psum,
     ):
         offsets = held.tile([P, N // 16], U16, name="offsets")
         nc.sync.dma_start(offsets[:], offs)
@@ -38,8 +39,8 @@ def tile_gather_matmul_kernel(tc, table, w, b, offs, out):
 
         pooled = held.tile([P, BLOCKS, V], F32, name="pooled")
         for a in range(BLOCKS):
-            width = N // HALVES
-            for h in range(HALVES):
+            width = N // QUARTERS
+            for h in range(QUARTERS):
                 y = psum.tile([P, width], F32, name="y")
                 nc.tensor.matmul(
                     y[:],

import concourse.mybir as mybir

BF16, F32, U16 = mybir.dt.bfloat16, mybir.dt.float32, mybir.dt.uint16

P = 128
S = 1024
M = 512
N = 512
D = 16
V = N // D
BLOCKS = M // P
QUARTERS = 4
PIECES = BLOCKS * QUARTERS
BANKS = 8

FLOPS = 2 * P * M * N


def tile_gather_matmul_kernel(tc, table, w, b, offs, out):
    nc = tc.nc
    with (
        tc.tile_pool(name="held", bufs=1) as held,
        tc.tile_pool(name="work", bufs=PIECES) as work,
        tc.psum_pool(name="psum", bufs=BANKS) as psum,
    ):
        offsets = held.tile([P, N // 16], U16, name="offsets")
        nc.sync.dma_start(offsets[:], offs)
        nodes = held.tile([P, S], BF16, name="nodes")
        nc.sync.dma_start(nodes[:], table)
        weights = held.tile([P, M], BF16, name="weights")
        nc.scalar.dma_start(weights[:], w)
        bias = held.tile([P, BLOCKS], F32, name="bias")
        with nc.allow_non_contiguous_dma(reason="512 single values, one to a partition and block"):
            nc.scalar.dma_start(bias[:], b.rearrange("(a p) o -> p (a o)", p=P))

        early = held.tile([P, 2], F32, name="early")
        nc.vector.memset(early[:, 0:1], 0.0)
        nc.scalar.activation(early[:, 1:2], early[:, 0:1], mybir.ActivationFunctionType.Silu)

        pooled = held.tile([P, BLOCKS, V], F32, name="pooled")
        for a in range(BLOCKS):
            width = N // QUARTERS
            for h in range(QUARTERS):
                y = psum.tile([P, width], F32, name="y")
                nc.tensor.matmul(
                    y[:],
                    weights[:, a * P : (a + 1) * P],
                    nodes[:].indirect(offsets[:, h * width // 16 : (h + 1) * width // 16]),
                    start=True,
                    stop=True,
                )
                z = work.tile([P, width], F32, name="z")
                nc.scalar.activation(
                    z[:], y[:], mybir.ActivationFunctionType.Silu, bias=bias[:, a : a + 1]
                )
                nc.vector.tensor_reduce(
                    pooled[:, a, h * width // D : (h + 1) * width // D],
                    z[:].rearrange("p (v t) -> p v t", t=D),
                    axis=mybir.AxisListType.X,
                    op=mybir.AluOpType.max,
                )
            nc.sync.dma_start(out[a * P : (a + 1) * P, :], pooled[:, a, :])
